import numpy as np, ml_dtypes
CORES = [52,68,84,180,196,212,308,324,340]
N = 9
TK = 512
WID = [512,320,256,320,256,192,384,64,512]
def setup_inputs(rng):
    return {"x": rng.standard_normal((N, 128, TK), dtype=np.float32).astype(ml_dtypes.bfloat16), "w1": (rng.standard_normal((N, 128, 128), dtype=np.float32) / 8).astype(ml_dtypes.bfloat16), "w2": (rng.standard_normal((N, 128, 128), dtype=np.float32) / 8).astype(ml_dtypes.bfloat16)}
def setup_inputs_big(rng):
    d = setup_inputs(rng)
    for k in ("x", "w1", "w2"): d[k] = (d[k].astype(np.float32) * 1024.0).astype(d[k].dtype)
    return d
def setup_inputs_small(rng):
    d = setup_inputs(rng)
    for k in ("x", "w1", "w2"): d[k] = (d[k].astype(np.float32) * (1 / 1024.0)).astype(d[k].dtype)
    return d
def setup_inputs_apart(rng):
    d = setup_inputs(rng)
    f = (10.0 ** rng.permutation(np.linspace(-1.5, 1.5, N))).astype(np.float32).reshape(N, 1, 1)
    for k in ("x", "w1", "w2"): d[k] = (d[k].astype(np.float32) * f).astype(d[k].dtype)
    return d
def whole(x, w1, w2):
    X, W1, W2 = x.astype(np.float64), w1.astype(np.float64), w2.astype(np.float64)
    y = np.zeros((N, 128, TK))
    for r in range(N):
        for j in range(N):
            y[r] += W2[j].T @ np.maximum(W1[j].T @ X[r], 0.0)
    return {"y": y.astype(ml_dtypes.bfloat16 if x.dtype != np.float64 else np.float64)}
def reference(x, w1, w2):
    o = whole(x, w1, w2)["y"].copy()
    for r in range(N):
        o[r][:, WID[r]:] = np.nan
    return {"y": o}

@@ -1,0 +1,256 @@
+from concourse.bass import DstId, RemoteDMATransfer
+from concourse.mybir import AluOpType
+
+NE = 9
+D = 128
+WC = 2 * D
+TK = 512
+
+SCRATCH = {
+    "wall": ("sbuf", [D, NE * WC], "bfloat16"),
+    "xs": ("sbuf", [D, TK], "bfloat16"),
+    "zero": ("sbuf", [D, TK], "bfloat16"),
+    "hs0": ("sbuf", [D, TK], "bfloat16"),
+    "hs1": ("sbuf", [D, TK], "bfloat16"),
+    "ys": ("sbuf", [D, TK], "bfloat16"),
+    "hp0": ("psum", [D, TK], "float32"),
+    "hp1": ("psum", [D, TK], "float32"),
+    "hp2": ("psum", [D, TK], "float32"),
+    "ya": ("psum", [D, TK], "float32"),
+    "yb": ("psum", [D, TK], "float32"),
+}
+SEMAPHORES = (["lw", "lx", "xa", "yr", "z", "sent", "pa", "pb", "ra", "rb", "qa", "qb", "oa", "ob", "sa", "sb"]
+              + ["a%d" % j for j in range(NE)] + ["p%d" % i for i in range(NE)]
+              + ["r%d" % i for i in range(NE)] + ["q%d" % i for i in range(NE)])
+
+HOP = 3.0
+
+
+def _plan(T, topo):
+    cores = list(T.cores)
+    wid = list(T.tables["WID"])
+    n = len(cores)
+    R = list(range(n))
+
+    def ok(a, b):
+        return topo.may_write(cores[a], cores[b])
+
+    def partner(r, group):
+        return [o for o in group if topo.chip(cores[o]) == topo.chip(cores[r])][0]
+
+    hub = [r for r in R if all(ok(r, o) and ok(o, r) for o in R if o != r)]
+    wings = {}
+    for r in R:
+        if r not in hub:
+            wings.setdefault(topo.host(cores[r]), []).append(r)
+    wings = [wings[h] for h in sorted(wings)]
+    deleg = {r: partner(r, hub) for r in R if r not in hub and 2 * wid[r] < WC}
+    hosts = {h: g for g, h in deleg.items()}
+    sites = [r for r in R if r not in deleg]
+
+    def heavy(ds):
+        return sorted(ds, key=lambda d: -wid[d] - (wid[hosts[d]] if d in hosts else 0))
+
+    def not_last(ds, k):
+        ds = heavy(ds)
+        if len(ds) > 2 and k % 2:
+            ds = ds[:-2] + [ds[-1], ds[-2]]
+        return ds
+
+    first = {}
+    fwd = {r: [] for r in R}
+    late = {r: [] for r in R}
+    for w in wings:
+        for o in w:
+            p = partner(o, hub)
+            rest = [h for h in hub if h != p]
+            near = [s for s in w if s in sites and s != o]
+            first[o] = [p] + [h for h in rest if h in hosts] + heavy(near)
+            late[o] = [h for h in rest if h not in hosts]
+            if len(first[o]) + len(late[o]) <= 1 + HOP:
+                first[o] += late[o]
+                late[o] = []
+            far = [s for s in sites if s != o and not ok(o, s)]
+            fwd[p].append((o, not_last(far, hub.index(p))))
+    for o in hub:
+        peers = [h for h in hub if h != o]
+        peers.sort(key=lambda h: (h not in hosts, (h - o) % n))
+        fs = []
+        for w in wings:
+            f = partner(o, w)
+            inrack = topo.rack(topo.host(cores[f])) == topo.rack(topo.host(cores[o]))
+            on = heavy([s for s in w if s in sites and s != f])
+            if inrack:
+                on = on + peers[1:]
+                fs.insert(0, f)
+            else:
+                fs.append(f)
+            if on:
+                fwd[f].append((o, on))
+        first[o] = fs + peers[:1]
+
+    land = {r: {r: -1.0} for r in R}
+    free = {}
+    prog = {}
+    for r in R:
+        t = 0.25 if r in deleg else 0.0
+        for d in first[r]:
+            t += 1.0
+            land[d][r] = t
+        free[r] = t
+    for r in R:
+        fwd[r].sort(key=lambda e: (land[r][e[0]], len(e[1])))
+        prog[r] = [(r, first[r])] + fwd[r] + ([(r, late[r])] if late[r] else [])
+        for j, ds in prog[r][1:]:
+            t = max(free[r], land[r][j] + HOP)
+            for d in ds:
+                t += 1.0
+                land[d][j] = t
+            free[r] = t
+    order = {s: sorted(land[s], key=lambda j: land[s][j]) for s in sites}
+    return {"cores": cores, "wid": wid, "deleg": deleg, "hosts": hosts, "sites": sites, "prog": prog, "order": order}
+
+
+def _bits(m):
+    return bin(m).count("1")
+
+
+def rank_program(g, core, T, topo):
+    rank = T.rank_of(core)
+    if rank is None:
+        return
+    P = _plan(T, topo)
+    cores, wid = P["cores"], P["wid"]
+    S = T.sem
+    te, ve, sy, sc = g.tensor, g.vector, g.sync, g.scalar
+    w = wid[rank]
+    guest = P["hosts"].get(rank)
+    gw = wid[guest] if guest is not None else 0
+    site = rank in P["sites"]
+
+    def slot(j):
+        return T.wall[:, j * WC:(j + 1) * WC]
+
+    def arrived(q, j):
+        if j == rank:
+            q.wait_ge(S.lw, 32)
+        else:
+            q.wait_ge(S["a%d" % j], 8)
+
+    if site:
+        sy.dma_start(T.wall[:, rank * WC:rank * WC + D], T.w1[:, :]).then_inc(S.lw, 16)
+        sc.dma_start(T.wall[:, rank * WC + D:(rank + 1) * WC], T.w2[:, :]).then_inc(S.lw, 16)
+        sy.dma_start(T.xs[:, gw:gw + w], T.x[:, 0:w]).then_inc(S.lx, 16)
+    else:
+        sy.dma_start(T.xs[:, 0:w], T.x[:, 0:w]).then_inc(S.lx, 16)
+        sc.dma_start(T.wall[:, rank * WC:rank * WC + D], T.w1[:, :]).then_inc(S.lw, 16)
+        sy.dma_start(T.wall[:, rank * WC + D:(rank + 1) * WC], T.w2[:, :]).then_inc(S.lw, 16)
+
+    sent = [0]
+
+    def one(dst, out_ap, in_ap, sem):
+        rid, pid = topo.addr(cores[dst], core)
+        m = topo.mask(core, cores[dst])
+        g.remote_dma(out_ap=out_ap, in_ap=in_ap, remote_sem=sem, local_sem=S.sent, pid=pid, routing_id=rid,
+                     dma_engine_mask=m)
+        sent[0] += _bits(m)
+
+    def spread(j, dsts):
+        m = topo.mask(core, cores[dsts[0]])
+        ids = []
+        for d in dsts:
+            m &= topo.mask(core, cores[d])
+            rid, pid = topo.addr(cores[d], core)
+            ids.append(DstId(rid=rid, pnc=pid))
+        g.remote_dma_fused([RemoteDMATransfer(dst_ids=ids, dma_engine_mask=m, remote_sem=S["a%d" % j],
+                                              srcs=[slot(j)], dsts=[slot(j) for _ in dsts], alu_op=0)],
+                           local_sem=S.sent)
+        sent[0] += _bits(m)
+
+    if not site:
+        g.wait_ge(S.lx, 16)
+        one(P["deleg"][rank], T.xs[:, 0:w], T.xs[:, 0:w], S.xa)
+    for j, dsts in P["prog"][rank]:
+        arrived(g, j)
+        spread(j, dsts)
+
+    if not site:
+        sy.wait_ge(S.yr, 8)
+        sy.dma_start(T.y[:, 0:w], T.ys[:, 0:w]).then_inc(S.sa, 16)
+        sy.wait_ge(S.sa, 16)
+        g.wait_ge(S.sent, sent[0])
+        return
+
+    n = gw + w
+    s = gw if gw else (n // 16) * 8
+    order = P["order"][rank]
+    last = len(order) - 1
+    hp = [T.hp0, T.hp1]
+    hs = [T.hs0, T.hs1]
+
+    def w1(j):
+        return T.wall[:, j * WC:j * WC + D]
+
+    def w2(j):
+        return T.wall[:, j * WC + D:(j + 1) * WC]
+
+    def mm1(i):
+        j = order[i]
+        arrived(te, j)
+        if i < last:
+            te.matmul(hp[i % 2][:, 0:n], w1(j), T.xs[:, 0:n], start=True, stop=True).then_inc(S["p%d" % i], 1)
+        else:
+            te.matmul(hp[i % 2][:, 0:s], w1(j), T.xs[:, 0:s], start=True, stop=True).then_inc(S.pa, 1)
+            te.matmul(T.hp2[:, 0:n - s], w1(j), T.xs[:, s:n], start=True, stop=True).then_inc(S.pb, 1)
+
+    def mm2(i):
+        j = order[i]
+        h = hs[i % 2]
+        if i < last:
+            te.wait_ge(S["r%d" % i], 1)
+            te.matmul(T.ya[:, 0:s], w2(j), h[:, 0:s], start=(i == 0), stop=False).then_inc(S["q%d" % i], 1)
+            te.matmul(T.yb[:, 0:n - s], w2(j), h[:, s:n], start=(i == 0), stop=False).then_inc(S["q%d" % i], 1)
+        else:
+            te.wait_ge(S.ra, 1)
+            te.matmul(T.ya[:, 0:s], w2(j), h[:, 0:s], start=False, stop=True).then_inc(S.qa, 1)
+            te.wait_ge(S.rb, 1)
+            te.matmul(T.yb[:, 0:n - s], w2(j), h[:, s:n], start=False, stop=True).then_inc(S.qb, 1)
+
+    te.wait_ge(S.lx, 16)
+    if gw:
+        te.wait_ge(S.xa, 8)
+    mm1(0)
+    for i in range(last):
+        mm1(i + 1)
+        mm2(i)
+    mm2(last)
+
+    ve.memset(T.zero[:, 0:n], 0.0).then_inc(S.z, 1)
+    ve.wait_ge(S.z, 1)
+    for i in range(last):
+        ve.wait_ge(S["p%d" % i], 1)
+        if i >= 2:
+            ve.wait_ge(S["q%d" % (i - 2)], 2)
+        ve.tensor_tensor(hs[i % 2][:, 0:n], hp[i % 2][:, 0:n], T.zero[:, 0:n], AluOpType.max).then_inc(S["r%d" % i], 1)
+    ve.wait_ge(S.pa, 1)
+    ve.wait_ge(S["q%d" % (last - 2)], 2)
+    ve.tensor_tensor(hs[last % 2][:, 0:s], hp[last % 2][:, 0:s], T.zero[:, 0:s], AluOpType.max).then_inc(S.ra, 1)
+    ve.wait_ge(S.pb, 1)
+    ve.tensor_tensor(hs[last % 2][:, s:n], T.hp2[:, 0:n - s], T.zero[:, s:n], AluOpType.max).then_inc(S.rb, 1)
+    ve.wait_ge(S["q%d" % (last - 1)], 2)
+    ve.wait_ge(S.qa, 1)
+    ve.tensor_copy(T.ys[:, 0:s], T.ya[:, 0:s]).then_inc(S.oa, 1)
+    ve.wait_ge(S.qb, 1)
+    ve.tensor_copy(T.ys[:, s:n], T.yb[:, 0:n - s]).then_inc(S.ob, 1)
+
+    if gw:
+        g.wait_ge(S.oa, 1)
+        one(guest, T.ys[:, 0:gw], T.ys[:, 0:gw], S.yr)
+    else:
+        sy.wait_ge(S.oa, 1)
+        sy.dma_start(T.y[:, 0:s], T.ys[:, 0:s]).then_inc(S.sa, 16)
+        sy.wait_ge(S.sa, 16)
+    sc.wait_ge(S.ob, 1)
+    sc.dma_start(T.y[:, s - gw:n - gw], T.ys[:, s:n]).then_inc(S.sb, 16)
+    sc.wait_ge(S.sb, 16)
+    g.wait_ge(S.sent, sent[0])

@@ -5,6 +5,7 @@ NE = 9
 D = 128
 WC = 2 * D
 TK = 512
+NHOSTS = 4
 
 SCRATCH = {
     "wall": ("sbuf", [D, NE * WC], "bfloat16"),
@@ -19,11 +20,12 @@ SCRATCH = {
     "ya": ("psum", [D, TK], "float32"),
     "yb": ("psum", [D, TK], "float32"),
 }
-SEMAPHORES = (["lw", "lx", "xa", "yr", "z", "sent", "pa", "pb", "ra", "rb", "qa", "qb", "oa", "ob", "sa", "sb"]
+SEMAPHORES = (["lw", "lx", "z", "sent", "pa", "pb", "ra", "rb", "qa", "qb", "oa", "ob", "sa", "sb"]
               + ["a%d" % j for j in range(NE)] + ["p%d" % i for i in range(NE)]
               + ["r%d" % i for i in range(NE)] + ["q%d" % i for i in range(NE)])
 
 HOP = 3.0
+COLD = 3.0
 
 
 def _plan(T, topo):
@@ -35,21 +37,14 @@ def _plan(T, topo):
     def ok(a, b):
         return topo.may_write(cores[a], cores[b])
 
+    def rack(c):
+        return topo.rack(topo.host(c))
+
     def partner(r, group):
         return [o for o in group if topo.chip(cores[o]) == topo.chip(cores[r])][0]
 
-    hub = [r for r in R if all(ok(r, o) and ok(o, r) for o in R if o != r)]
-    wings = {}
-    for r in R:
-        if r not in hub:
-            wings.setdefault(topo.host(cores[r]), []).append(r)
-    wings = [wings[h] for h in sorted(wings)]
-    deleg = {r: partner(r, hub) for r in R if r not in hub and 2 * wid[r] < WC}
-    hosts = {h: g for g, h in deleg.items()}
-    sites = [r for r in R if r not in deleg]
-
     def heavy(ds):
-        return sorted(ds, key=lambda d: -wid[d] - (wid[hosts[d]] if d in hosts else 0))
+        return sorted(ds, key=lambda d: -wid[d])
 
     def not_last(ds, k):
         ds = heavy(ds)
@@ -57,58 +52,68 @@ def _plan(T, topo):
             ds = ds[:-2] + [ds[-1], ds[-2]]
         return ds
 
+    hub = [r for r in R if all(ok(r, o) and ok(o, r) for o in R if o != r)]
+    wings = {}
+    for r in R:
+        if r not in hub:
+            wings.setdefault(topo.host(cores[r]), []).append(r)
+    wings = [wings[h] for h in sorted(wings)]
+
     first = {}
     fwd = {r: [] for r in R}
     late = {r: [] for r in R}
     for w in wings:
         for o in w:
-            p = partner(o, hub)
-            rest = [h for h in hub if h != p]
-            near = [s for s in w if s in sites and s != o]
-            first[o] = [p] + [h for h in rest if h in hosts] + heavy(near)
-            late[o] = [h for h in rest if h not in hosts]
-            if len(first[o]) + len(late[o]) <= 1 + HOP:
-                first[o] += late[o]
-                late[o] = []
-            far = [s for s in sites if s != o and not ok(o, s)]
-            fwd[p].append((o, not_last(far, hub.index(p))))
+            near = heavy([s for s in w if s != o])
+            far = [s for s in R if s != o and not ok(o, s)]
+            if rack(cores[o]) == rack(cores[hub[0]]):
+                c0 = cores[o]
+                cand = [c for c in range(NHOSTS * topo.CORES_PER_HOST)
+                        if T.rank_of(c) is None and topo.chip(c) == topo.chip(c0) and rack(c) == rack(cores[far[0]])
+                        and topo.die(c) == topo.die(cores[far[0]]) and topo.may_write(c0, c)
+                        and all(topo.may_write(c, cores[s]) for s in far)]
+                h = len(cores)
+                cores.append(cand[0])
+                fwd[h] = [(o, heavy(far))]
+                first[o] = [h] + near
+                late[o] = heavy(hub)
+            else:
+                p = partner(o, hub)
+                first[o] = [p] + near
+                fwd[p].append((o, not_last(far, hub.index(p)) + heavy([h for h in hub if h != p])))
     for o in hub:
-        peers = [h for h in hub if h != o]
-        peers.sort(key=lambda h: (h not in hosts, (h - o) % n))
         fs = []
         for w in wings:
             f = partner(o, w)
-            inrack = topo.rack(topo.host(cores[f])) == topo.rack(topo.host(cores[o]))
-            on = heavy([s for s in w if s in sites and s != f])
-            if inrack:
-                on = on + peers[1:]
+            if rack(cores[f]) == rack(cores[o]):
                 fs.insert(0, f)
             else:
                 fs.append(f)
-            if on:
-                fwd[f].append((o, on))
-        first[o] = fs + peers[:1]
+            fwd[f].append((o, heavy([s for s in w if s != f])))
+        first[o] = fs + heavy([h for h in hub if h != o])
 
-    land = {r: {r: -1.0} for r in R}
-    free = {}
+    nodes = list(range(len(cores)))
+    land = {v: {} for v in nodes}
+    free = {v: 0.0 for v in nodes}
     prog = {}
     for r in R:
-        t = 0.25 if r in deleg else 0.0
+        land[r][r] = -1.0
+        t = 0.0
         for d in first[r]:
             t += 1.0
             land[d][r] = t
         free[r] = t
-    for r in R:
-        fwd[r].sort(key=lambda e: (land[r][e[0]], len(e[1])))
-        prog[r] = [(r, first[r])] + fwd[r] + ([(r, late[r])] if late[r] else [])
-        for j, ds in prog[r][1:]:
-            t = max(free[r], land[r][j] + HOP)
+    for v in nodes:
+        fwd[v].sort(key=lambda e: (land[v][e[0]], len(e[1])))
+        prog[v] = fwd[v] if v >= n else [(v, first[v])] + fwd[v] + ([(v, late[v])] if late[v] else [])
+        for j, ds in (prog[v] if v >= n else prog[v][1:]):
+            t = max(free[v], land[v][j] + HOP + (COLD if v >= n else 0.0))
             for d in ds:
                 t += 1.0
                 land[d][j] = t
-            free[r] = t
-    order = {s: sorted(land[s], key=lambda j: land[s][j]) for s in sites}
-    return {"cores": cores, "wid": wid, "deleg": deleg, "hosts": hosts, "sites": sites, "prog": prog, "order": order}
+            free[v] = t
+    order = {s: sorted(land[s], key=lambda j: land[s][j]) for s in R}
+    return {"cores": cores, "wid": wid, "prog": prog, "order": order}
 
 
 def _bits(m):
@@ -117,16 +122,16 @@ def _bits(m):
 
 def rank_program(g, core, T, topo):
     rank = T.rank_of(core)
-    if rank is None:
+    if rank is None and topo.host(core) in [topo.host(c) for c in T.cores]:
         return
     P = _plan(T, topo)
     cores, wid = P["cores"], P["wid"]
+    if core not in cores:
+        return
+    node = cores.index(core)
     S = T.sem
     te, ve, sy, sc = g.tensor, g.vector, g.sync, g.scalar
-    w = wid[rank]
-    guest = P["hosts"].get(rank)
-    gw = wid[guest] if guest is not None else 0
-    site = rank in P["sites"]
+    ne = max(_bits(topo.mask(c, core)) for c in cores if c != core)
 
     def slot(j):
         return T.wall[:, j * WC:(j + 1) * WC]
@@ -135,27 +140,17 @@ def rank_program(g, core, T, topo):
         if j == rank:
             q.wait_ge(S.lw, 32)
         else:
-            q.wait_ge(S["a%d" % j], 8)
+            q.wait_ge(S["a%d" % j], ne)
 
-    if site:
+    if rank is not None:
+        w = wid[rank]
         sy.dma_start(T.wall[:, rank * WC:rank * WC + D], T.w1[:, :]).then_inc(S.lw, 16)
         sc.dma_start(T.wall[:, rank * WC + D:(rank + 1) * WC], T.w2[:, :]).then_inc(S.lw, 16)
-        sy.dma_start(T.xs[:, gw:gw + w], T.x[:, 0:w]).then_inc(S.lx, 16)
-    else:
         sy.dma_start(T.xs[:, 0:w], T.x[:, 0:w]).then_inc(S.lx, 16)
-        sc.dma_start(T.wall[:, rank * WC:rank * WC + D], T.w1[:, :]).then_inc(S.lw, 16)
-        sy.dma_start(T.wall[:, rank * WC + D:(rank + 1) * WC], T.w2[:, :]).then_inc(S.lw, 16)
 
-    sent = [0]
-
-    def one(dst, out_ap, in_ap, sem):
-        rid, pid = topo.addr(cores[dst], core)
-        m = topo.mask(core, cores[dst])
-        g.remote_dma(out_ap=out_ap, in_ap=in_ap, remote_sem=sem, local_sem=S.sent, pid=pid, routing_id=rid,
-                     dma_engine_mask=m)
-        sent[0] += _bits(m)
-
-    def spread(j, dsts):
+    sent = 0
+    for j, dsts in P["prog"][node]:
+        arrived(g, j)
         m = topo.mask(core, cores[dsts[0]])
         ids = []
         for d in dsts:
@@ -165,24 +160,13 @@ def rank_program(g, core, T, topo):
         g.remote_dma_fused([RemoteDMATransfer(dst_ids=ids, dma_engine_mask=m, remote_sem=S["a%d" % j],
                                               srcs=[slot(j)], dsts=[slot(j) for _ in dsts], alu_op=0)],
                            local_sem=S.sent)
-        sent[0] += _bits(m)
-
-    if not site:
-        g.wait_ge(S.lx, 16)
-        one(P["deleg"][rank], T.xs[:, 0:w], T.xs[:, 0:w], S.xa)
-    for j, dsts in P["prog"][rank]:
-        arrived(g, j)
-        spread(j, dsts)
-
-    if not site:
-        sy.wait_ge(S.yr, 8)
-        sy.dma_start(T.y[:, 0:w], T.ys[:, 0:w]).then_inc(S.sa, 16)
-        sy.wait_ge(S.sa, 16)
-        g.wait_ge(S.sent, sent[0])
+        sent += _bits(m)
+    if rank is None:
+        g.wait_ge(S.sent, sent)
         return
 
-    n = gw + w
-    s = gw if gw else (n // 16) * 8
+    n = w
+    s = (n // 16) * 8
     order = P["order"][rank]
     last = len(order) - 1
     hp = [T.hp0, T.hp1]
@@ -217,8 +201,6 @@ def rank_program(g, core, T, topo):
             te.matmul(T.yb[:, 0:n - s], w2(j), h[:, s:n], start=False, stop=True).then_inc(S.qb, 1)
 
     te.wait_ge(S.lx, 16)
-    if gw:
-        te.wait_ge(S.xa, 8)
     mm1(0)
     for i in range(last):
         mm1(i + 1)
@@ -243,14 +225,10 @@ def rank_program(g, core, T, topo):
     ve.wait_ge(S.qb, 1)
     ve.tensor_copy(T.ys[:, s:n], T.yb[:, 0:n - s]).then_inc(S.ob, 1)
 
-    if gw:
-        g.wait_ge(S.oa, 1)
-        one(guest, T.ys[:, 0:gw], T.ys[:, 0:gw], S.yr)
-    else:
-        sy.wait_ge(S.oa, 1)
-        sy.dma_start(T.y[:, 0:s], T.ys[:, 0:s]).then_inc(S.sa, 16)
-        sy.wait_ge(S.sa, 16)
+    sy.wait_ge(S.oa, 1)
+    sy.dma_start(T.y[:, 0:s], T.ys[:, 0:s]).then_inc(S.sa, 16)
+    sy.wait_ge(S.sa, 16)
     sc.wait_ge(S.ob, 1)
-    sc.dma_start(T.y[:, s - gw:n - gw], T.ys[:, s:n]).then_inc(S.sb, 16)
+    sc.dma_start(T.y[:, s:n], T.ys[:, s:n]).then_inc(S.sb, 16)
     sc.wait_ge(S.sb, 16)
-    g.wait_ge(S.sent, sent[0])
+    g.wait_ge(S.sent, sent)

@@ -14,18 +14,25 @@ SCRATCH = {
     "hs0": ("sbuf", [D, TK], "bfloat16"),
     "hs1": ("sbuf", [D, TK], "bfloat16"),
     "ys": ("sbuf", [D, TK], "bfloat16"),
+    "pr": ("sbuf", [D, TK], "bfloat16"),
     "hp0": ("psum", [D, TK], "float32"),
     "hp1": ("psum", [D, TK], "float32"),
     "hp2": ("psum", [D, TK], "float32"),
     "ya": ("psum", [D, TK], "float32"),
     "yb": ("psum", [D, TK], "float32"),
 }
-SEMAPHORES = (["lw", "lx", "z", "sent", "pa", "pb", "ra", "rb", "qa", "qb", "oa", "ob", "sa", "sb"]
-              + ["a%d" % j for j in range(NE)] + ["p%d" % i for i in range(NE)]
+SEMAPHORES = (["lw", "lx", "xr", "z", "sent", "pa", "pb", "ra", "rb", "qa", "qb", "oa", "ob", "sa", "sb", "reta", "retb"]
+              + ["a%d" % j for j in range(NE)] + ["b%d" % j for j in range(NE)] + ["p%d" % i for i in range(NE)]
               + ["r%d" % i for i in range(NE)] + ["q%d" % i for i in range(NE)])
 
-HOP = 3.0
-COLD = 3.0
+HOP = 1.0
+COLD = 2.0
+CABLE = 2.5
+CHIP = 0.5
+HALF = 0.6
+LANE = 1.6
+
+_CACHE = {}
 
 
 def _plan(T, topo):
@@ -40,17 +47,19 @@ def _plan(T, topo):
     def rack(c):
         return topo.rack(topo.host(c))
 
+    def place(c):
+        return (topo.host(c), topo.chip(c))
+
     def partner(r, group):
         return [o for o in group if topo.chip(cores[o]) == topo.chip(cores[r])][0]
 
     def heavy(ds):
         return sorted(ds, key=lambda d: -wid[d])
 
-    def not_last(ds, k):
-        ds = heavy(ds)
-        if len(ds) > 2 and k % 2:
-            ds = ds[:-2] + [ds[-1], ds[-2]]
-        return ds
+    def idle(pred):
+        c = [c for c in range(NHOSTS * topo.CORES_PER_HOST) if T.rank_of(c) is None and c not in cores and pred(c)][0]
+        cores.append(c)
+        return len(cores) - 1
 
     hub = [r for r in R if all(ok(r, o) and ok(o, r) for o in R if o != r)]
     wings = {}
@@ -59,61 +68,95 @@ def _plan(T, topo):
             wings.setdefault(topo.host(cores[r]), []).append(r)
     wings = [wings[h] for h in sorted(wings)]
 
-    first = {}
-    fwd = {r: [] for r in R}
-    late = {r: [] for r in R}
+    aide, home, gives = {}, {}, {}
+    for w in wings:
+        for r in w:
+            if wid[r] * NE > max(wid) * (NE - len(w) + 1):
+                c0 = cores[r]
+                aide[r] = idle(lambda c: place(c) == place(c0) and topo.die(c) == topo.die(c0))
+                home[aide[r]] = r
+                gives[r] = [s for s in w if s != r]
+
+    def worker(s, j):
+        return aide[s] if s in aide and j in gives[s] else s
+
+    own = {r: [] for r in R}
+    fwd = {v: [] for v in range(len(cores))}
     for w in wings:
         for o in w:
-            near = heavy([s for s in w if s != o])
-            far = [s for s in R if s != o and not ok(o, s)]
-            if rack(cores[o]) == rack(cores[hub[0]]):
-                c0 = cores[o]
-                cand = [c for c in range(NHOSTS * topo.CORES_PER_HOST)
-                        if T.rank_of(c) is None and topo.chip(c) == topo.chip(c0) and rack(c) == rack(cores[far[0]])
-                        and topo.die(c) == topo.die(cores[far[0]]) and topo.may_write(c0, c)
-                        and all(topo.may_write(c, cores[s]) for s in far)]
-                h = len(cores)
-                cores.append(cand[0])
-                fwd[h] = [(o, heavy(far))]
-                first[o] = [h] + near
-                late[o] = heavy(hub)
+            c0 = cores[o]
+            near = [worker(s, o) for s in heavy([s for s in w if s != o])]
+            far = heavy([s for s in R if s != o and not ok(o, s)])
+            inrack = rack(c0) == rack(cores[hub[0]])
+            p = partner(o, hub)
+            rl = idle(lambda c: topo.chip(c) == topo.chip(c0) and rack(c) != rack(c0) and topo.die(c) != topo.die(c0)
+                      and topo.may_write(c0, c) and all(topo.may_write(c, cores[s]) for s in far)
+                      and (inrack or place(c) == place(cores[p])))
+            own[o] = [("a", o, [rl], "C"), ("b", o, [rl], "C")]
+            fwd[rl] = [("a", o, far, "C"), ("b", o, far, "S")]
+            if inrack:
+                own[o].append(("f", o, [p] + near, "S"))
             else:
-                p = partner(o, hub)
-                first[o] = [p] + near
-                fwd[p].append((o, not_last(far, hub.index(p)) + heavy([h for h in hub if h != p])))
+                own[o].append(("f", o, near, "S"))
+                fwd[rl].append(("f", o, [p], "H"))
+            fwd[p].append(("f", o, heavy([h for h in hub if h != p]), "L"))
     for o in hub:
-        fs = []
+        first = []
         for w in wings:
             f = partner(o, w)
+            k = worker(f, o)
+            rest = heavy([s for s in w if s != f])
             if rack(cores[f]) == rack(cores[o]):
-                fs.insert(0, f)
+                first.append(k)
+                fwd[k].append(("f", o, rest, "L"))
             else:
-                fs.append(f)
-            fwd[f].append((o, heavy([s for s in w if s != f])))
-        first[o] = fs + heavy([h for h in hub if h != o])
+                own[o] += [("a", o, [k], "C"), ("b", o, [k], "C")]
+                fwd[k] += [("a", o, rest, "C"), ("b", o, rest, "S")]
+        own[o].append(("f", o, first + heavy([h for h in hub if h != o]), "S"))
 
     nodes = list(range(len(cores)))
-    land = {v: {} for v in nodes}
-    free = {v: 0.0 for v in nodes}
     prog = {}
-    for r in R:
-        land[r][r] = -1.0
-        t = 0.0
-        for d in first[r]:
-            t += 1.0
-            land[d][r] = t
-        free[r] = t
     for v in nodes:
-        fwd[v].sort(key=lambda e: (land[v][e[0]], len(e[1])))
-        prog[v] = fwd[v] if v >= n else [(v, first[v])] + fwd[v] + ([(v, late[v])] if late[v] else [])
-        for j, ds in (prog[v] if v >= n else prog[v][1:]):
-            t = max(free[v], land[v][j] + HOP + (COLD if v >= n else 0.0))
-            for d in ds:
-                t += 1.0
-                land[d][j] = t
-            free[v] = t
-    order = {s: sorted(land[s], key=lambda j: land[s][j]) for s in R}
-    return {"cores": cores, "wid": wid, "prog": prog, "order": order}
+        prog[v] = own.get(v, []) + ([("x", None, [aide[v]], "H")] if v in aide else []) + fwd.get(v, [])
+
+    def cost(a, b, kind, lane):
+        ca, cb = cores[a], cores[b]
+        full = CABLE if rack(ca) != rack(cb) else (CHIP if place(ca) == place(cb) else 1.0) * (1.0 if lane == "L" else LANE)
+        return full if kind == "f" else full * HALF
+
+    land = {v: {} for v in nodes}
+    got = {v: {} for v in nodes}
+    for r in R:
+        land[r][(r, "a")] = land[r][(r, "b")] = -HOP
+    ptr = {v: 0 for v in nodes}
+    free = {(v, l): 0.0 for v in nodes for l in "CSH"}
+    moved = True
+    while moved:
+        moved = False
+        for v in nodes:
+            while ptr[v] < len(prog[v]):
+                kind, j, ds, lane = prog[v][ptr[v]]
+                if kind != "x":
+                    ls = "CS" if lane == "L" else lane
+                    need = ["a", "b"] if kind == "f" else [kind]
+                    if any((j, p) not in land[v] for p in need):
+                        break
+                    t = max(land[v][(j, p)] for p in need) + HOP + (COLD if v >= n and ptr[v] == 0 else 0.0)
+                    t = max([t] + [free[(v, l)] for l in ls])
+                    for d in ds:
+                        t += cost(v, d, kind, lane)
+                        for p in need:
+                            land[d][(j, p)] = t
+                        got[d].setdefault(j, {})[kind] = (v, lane)
+                    for l in ls:
+                        free[(v, l)] = t
+                ptr[v] += 1
+                moved = True
+    order = {}
+    for v in R + list(home):
+        js = [j for j in range(NE) if (j, "b") in land[v]]
+        order[v] = sorted(js, key=lambda j: land[v][(j, "b")])
+    return {"cores": cores, "wid": wid, "prog": prog, "order": order, "got": got, "aide": aide, "home": home}
 
 
 def _bits(m):
@@ -121,26 +164,67 @@ def _bits(m):
 
 
 def rank_program(g, core, T, topo):
-    rank = T.rank_of(core)
-    if rank is None and topo.host(core) in [topo.host(c) for c in T.cores]:
-        return
-    P = _plan(T, topo)
+    if "p" not in _CACHE:
+        _CACHE["p"] = _plan(T, topo)
+    P = _CACHE["p"]
     cores, wid = P["cores"], P["wid"]
     if core not in cores:
         return
     node = cores.index(core)
+    rank = T.rank_of(core)
+    home = P["home"].get(node)
     S = T.sem
     te, ve, sy, sc = g.tensor, g.vector, g.sync, g.scalar
-    ne = max(_bits(topo.mask(c, core)) for c in cores if c != core)
 
-    def slot(j):
-        return T.wall[:, j * WC:(j + 1) * WC]
+    def lanes(c):
+        ms = [topo.mask(c, o) for o in cores if o != c and topo.mask(c, o)]
+        lo, al = ms[0], ms[0]
+        for m in ms:
+            lo &= m
+            al |= m
+        return lo, al & ~lo
 
-    def arrived(q, j):
+    def lane(c, tag):
+        lo, hi = lanes(c)
+        if tag == "L":
+            return lo
+        if tag == "H":
+            return hi
+        bs = [b for b in range(lo.bit_length()) if (lo >> b) & 1]
+        return sum(1 << b for b in (bs[0::2] if tag == "C" else bs[1::2]))
+
+    got = P["got"][node]
+
+    def adds(j, kind):
+        v, tag = got[j][kind]
+        return _bits(lane(cores[v], tag))
+
+    def piece(j, kind):
+        a = j * WC + (D if kind == "b" else 0)
+        b = j * WC + (D if kind == "a" else WC)
+        return T.wall[:, a:b]
+
+    def arrived(q, j, kind):
         if j == rank:
             q.wait_ge(S.lw, 32)
+        elif "f" in got[j]:
+            q.wait_ge(S["a%d" % j], adds(j, "f"))
         else:
-            q.wait_ge(S["a%d" % j], ne)
+            if kind != "b":
+                q.wait_ge(S["a%d" % j], adds(j, "a"))
+            if kind != "a":
+                q.wait_ge(S["b%d" % j], adds(j, "b"))
+
+    sent = [0]
+
+    def put(src, dst, dsts, sem, m):
+        ids = []
+        for d in dsts:
+            rid, pid = topo.addr(cores[d], core)
+            ids.append(DstId(rid=rid, pnc=pid))
+        g.remote_dma_fused([RemoteDMATransfer(dst_ids=ids, dma_engine_mask=m, remote_sem=sem,
+                                              srcs=[src], dsts=[dst for _ in dsts], alu_op=0)], local_sem=S.sent)
+        sent[0] += _bits(m)
 
     if rank is not None:
         w = wid[rank]
@@ -148,59 +232,52 @@ def rank_program(g, core, T, topo):
         sc.dma_start(T.wall[:, rank * WC + D:(rank + 1) * WC], T.w2[:, :]).then_inc(S.lw, 16)
         sy.dma_start(T.xs[:, 0:w], T.x[:, 0:w]).then_inc(S.lx, 16)
 
-    sent = 0
-    for j, dsts in P["prog"][node]:
-        arrived(g, j)
-        m = topo.mask(core, cores[dsts[0]])
-        ids = []
-        for d in dsts:
-            m &= topo.mask(core, cores[d])
-            rid, pid = topo.addr(cores[d], core)
-            ids.append(DstId(rid=rid, pnc=pid))
-        g.remote_dma_fused([RemoteDMATransfer(dst_ids=ids, dma_engine_mask=m, remote_sem=S["a%d" % j],
-                                              srcs=[slot(j)], dsts=[slot(j) for _ in dsts], alu_op=0)],
-                           local_sem=S.sent)
-        sent += _bits(m)
-    if rank is None:
-        g.wait_ge(S.sent, sent)
+    for kind, j, dsts, tag in P["prog"][node]:
+        if kind == "x":
+            g.wait_ge(S.lx, 16)
+            put(T.xs[:, 0:w], T.xs[:, 0:w], dsts, S.xr, lane(core, tag))
+        else:
+            arrived(g, j, kind)
+            put(piece(j, kind), piece(j, kind), dsts, S[("b%d" if kind == "b" else "a%d") % j], lane(core, tag))
+    if rank is None and home is None:
+        g.wait_ge(S.sent, sent[0])
         return
 
-    n = w
+    n = wid[rank] if rank is not None else wid[home]
     s = (n // 16) * 8
-    order = P["order"][rank]
+    order = P["order"][node]
     last = len(order) - 1
     hp = [T.hp0, T.hp1]
     hs = [T.hs0, T.hs1]
 
-    def w1(j):
-        return T.wall[:, j * WC:j * WC + D]
-
-    def w2(j):
-        return T.wall[:, j * WC + D:(j + 1) * WC]
-
     def mm1(i):
         j = order[i]
-        arrived(te, j)
+        arrived(te, j, "a")
         if i < last:
-            te.matmul(hp[i % 2][:, 0:n], w1(j), T.xs[:, 0:n], start=True, stop=True).then_inc(S["p%d" % i], 1)
+            te.matmul(hp[i % 2][:, 0:n], piece(j, "a"), T.xs[:, 0:n], start=True, stop=True).then_inc(S["p%d" % i], 1)
         else:
-            te.matmul(hp[i % 2][:, 0:s], w1(j), T.xs[:, 0:s], start=True, stop=True).then_inc(S.pa, 1)
-            te.matmul(T.hp2[:, 0:n - s], w1(j), T.xs[:, s:n], start=True, stop=True).then_inc(S.pb, 1)
+            te.matmul(hp[i % 2][:, 0:s], piece(j, "a"), T.xs[:, 0:s], start=True, stop=True).then_inc(S.pa, 1)
+            te.matmul(T.hp2[:, 0:n - s], piece(j, "a"), T.xs[:, s:n], start=True, stop=True).then_inc(S.pb, 1)
 
     def mm2(i):
         j = order[i]
         h = hs[i % 2]
+        if j != rank and "f" not in got[j]:
+            arrived(te, j, "b")
         if i < last:
             te.wait_ge(S["r%d" % i], 1)
-            te.matmul(T.ya[:, 0:s], w2(j), h[:, 0:s], start=(i == 0), stop=False).then_inc(S["q%d" % i], 1)
-            te.matmul(T.yb[:, 0:n - s], w2(j), h[:, s:n], start=(i == 0), stop=False).then_inc(S["q%d" % i], 1)
+            te.matmul(T.ya[:, 0:s], piece(j, "b"), h[:, 0:s], start=(i == 0), stop=False).then_inc(S["q%d" % i], 1)
+            te.matmul(T.yb[:, 0:n - s], piece(j, "b"), h[:, s:n], start=(i == 0), stop=False).then_inc(S["q%d" % i], 1)
         else:
             te.wait_ge(S.ra, 1)
-            te.matmul(T.ya[:, 0:s], w2(j), h[:, 0:s], start=False, stop=True).then_inc(S.qa, 1)
+            te.matmul(T.ya[:, 0:s], piece(j, "b"), h[:, 0:s], start=False, stop=True).then_inc(S.qa, 1)
             te.wait_ge(S.rb, 1)
-            te.matmul(T.yb[:, 0:n - s], w2(j), h[:, s:n], start=False, stop=True).then_inc(S.qb, 1)
+            te.matmul(T.yb[:, 0:n - s], piece(j, "b"), h[:, s:n], start=False, stop=True).then_inc(S.qb, 1)
 
-    te.wait_ge(S.lx, 16)
+    if rank is not None:
+        te.wait_ge(S.lx, 16)
+    else:
+        te.wait_ge(S.xr, _bits(lane(cores[home], "H")))
     mm1(0)
     for i in range(last):
         mm1(i + 1)
@@ -215,15 +292,33 @@ def rank_program(g, core, T, topo):
             ve.wait_ge(S["q%d" % (i - 2)], 2)
         ve.tensor_tensor(hs[i % 2][:, 0:n], hp[i % 2][:, 0:n], T.zero[:, 0:n], AluOpType.max).then_inc(S["r%d" % i], 1)
     ve.wait_ge(S.pa, 1)
-    ve.wait_ge(S["q%d" % (last - 2)], 2)
+    if last >= 2:
+        ve.wait_ge(S["q%d" % (last - 2)], 2)
     ve.tensor_tensor(hs[last % 2][:, 0:s], hp[last % 2][:, 0:s], T.zero[:, 0:s], AluOpType.max).then_inc(S.ra, 1)
     ve.wait_ge(S.pb, 1)
     ve.tensor_tensor(hs[last % 2][:, s:n], T.hp2[:, 0:n - s], T.zero[:, s:n], AluOpType.max).then_inc(S.rb, 1)
     ve.wait_ge(S["q%d" % (last - 1)], 2)
+    helped = rank is not None and rank in P["aide"]
     ve.wait_ge(S.qa, 1)
-    ve.tensor_copy(T.ys[:, 0:s], T.ya[:, 0:s]).then_inc(S.oa, 1)
+    if helped:
+        ve.wait_ge(S.reta, _bits(lane(cores[P["aide"][rank]], "C")))
+        ve.tensor_tensor(T.ys[:, 0:s], T.ya[:, 0:s], T.pr[:, 0:s], AluOpType.add).then_inc(S.oa, 1)
+    else:
+        ve.tensor_copy(T.ys[:, 0:s], T.ya[:, 0:s]).then_inc(S.oa, 1)
     ve.wait_ge(S.qb, 1)
-    ve.tensor_copy(T.ys[:, s:n], T.yb[:, 0:n - s]).then_inc(S.ob, 1)
+    if helped:
+        ve.wait_ge(S.retb, _bits(lane(cores[P["aide"][rank]], "S")))
+        ve.tensor_tensor(T.ys[:, s:n], T.yb[:, 0:n - s], T.pr[:, s:n], AluOpType.add).then_inc(S.ob, 1)
+    else:
+        ve.tensor_copy(T.ys[:, s:n], T.yb[:, 0:n - s]).then_inc(S.ob, 1)
+
+    if rank is None:
+        g.wait_ge(S.oa, 1)
+        put(T.ys[:, 0:s], T.pr[:, 0:s], [home], S.reta, lane(core, "C"))
+        g.wait_ge(S.ob, 1)
+        put(T.ys[:, s:n], T.pr[:, s:n], [home], S.retb, lane(core, "S"))
+        g.wait_ge(S.sent, sent[0])
+        return
 
     sy.wait_ge(S.oa, 1)
     sy.dma_start(T.y[:, 0:s], T.ys[:, 0:s]).then_inc(S.sa, 16)
@@ -231,4 +326,4 @@ def rank_program(g, core, T, topo):
     sc.wait_ge(S.ob, 1)
     sc.dma_start(T.y[:, s:n], T.ys[:, s:n]).then_inc(S.sb, 16)
     sc.wait_ge(S.sb, 16)
-    g.wait_ge(S.sent, sent)
+    g.wait_ge(S.sent, sent[0])

from concourse.bass import DstId, RemoteDMATransfer
from concourse.mybir import AluOpType

NE = 9
D = 128
WC = 2 * D
TK = 512
NHOSTS = 4

SCRATCH = {
    "wall": ("sbuf", [D, NE * WC], "bfloat16"),
    "xs": ("sbuf", [D, TK], "bfloat16"),
    "zero": ("sbuf", [D, TK], "bfloat16"),
    "hs0": ("sbuf", [D, TK], "bfloat16"),
    "hs1": ("sbuf", [D, TK], "bfloat16"),
    "ys": ("sbuf", [D, TK], "bfloat16"),
    "pr": ("sbuf", [D, TK], "bfloat16"),
    "hp0": ("psum", [D, TK], "float32"),
    "hp1": ("psum", [D, TK], "float32"),
    "hp2": ("psum", [D, TK], "float32"),
    "ya": ("psum", [D, TK], "float32"),
    "yb": ("psum", [D, TK], "float32"),
}
SEMAPHORES = (["lw", "lx", "xr", "z", "sent", "pa", "pb", "ra", "rb", "qa", "qb", "oa", "ob", "sa", "sb", "reta", "retb"]
              + ["a%d" % j for j in range(NE)] + ["b%d" % j for j in range(NE)] + ["p%d" % i for i in range(NE)]
              + ["r%d" % i for i in range(NE)] + ["q%d" % i for i in range(NE)])

HOP = 1.0
COLD = 2.0
CABLE = 2.5
CHIP = 0.5
HALF = 0.6
LANE = 1.6

_CACHE = {}


def _plan(T, topo):
    cores = list(T.cores)
    wid = list(T.tables["WID"])
    n = len(cores)
    R = list(range(n))

    def ok(a, b):
        return topo.may_write(cores[a], cores[b])

    def rack(c):
        return topo.rack(topo.host(c))

    def place(c):
        return (topo.host(c), topo.chip(c))

    def partner(r, group):
        return [o for o in group if topo.chip(cores[o]) == topo.chip(cores[r])][0]

    def heavy(ds):
        return sorted(ds, key=lambda d: -wid[d])

    def idle(pred):
        c = [c for c in range(NHOSTS * topo.CORES_PER_HOST) if T.rank_of(c) is None and c not in cores and pred(c)][0]
        cores.append(c)
        return len(cores) - 1

    hub = [r for r in R if all(ok(r, o) and ok(o, r) for o in R if o != r)]
    wings = {}
    for r in R:
        if r not in hub:
            wings.setdefault(topo.host(cores[r]), []).append(r)
    wings = [wings[h] for h in sorted(wings)]

    aide, home, gives = {}, {}, {}
    for w in wings:
        for r in w:
            if wid[r] * NE > max(wid) * (NE - len(w) + 1):
                c0 = cores[r]
                aide[r] = idle(lambda c: place(c) == place(c0) and topo.die(c) == topo.die(c0))
                home[aide[r]] = r
                gives[r] = [s for s in w if s != r]

    def worker(s, j):
        return aide[s] if s in aide and j in gives[s] else s

    own = {r: [] for r in R}
    fwd = {v: [] for v in range(len(cores))}
    for w in wings:
        for o in w:
            c0 = cores[o]
            near = [worker(s, o) for s in heavy([s for s in w if s != o])]
            far = heavy([s for s in R if s != o and not ok(o, s)])
            inrack = rack(c0) == rack(cores[hub[0]])
            p = partner(o, hub)
            rl = idle(lambda c: topo.chip(c) == topo.chip(c0) and rack(c) != rack(c0) and topo.die(c) != topo.die(c0)
                      and topo.may_write(c0, c) and all(topo.may_write(c, cores[s]) for s in far)
                      and (inrack or place(c) == place(cores[p])))
            own[o] = [("a", o, [rl], "C"), ("b", o, [rl], "C")]
            fwd[rl] = [("a", o, far, "C"), ("b", o, far, "S")]
            if inrack:
                own[o].append(("f", o, [p] + near, "S"))
            else:
                own[o].append(("f", o, near, "S"))
                fwd[rl].append(("f", o, [p], "H"))
            fwd[p].append(("f", o, heavy([h for h in hub if h != p]), "L"))
    for o in hub:
        first = []
        for w in wings:
            f = partner(o, w)
            k = worker(f, o)
            rest = heavy([s for s in w if s != f])
            if rack(cores[f]) == rack(cores[o]):
                first.append(k)
                fwd[k].append(("f", o, rest, "L"))
            else:
                own[o] += [("a", o, [k], "C"), ("b", o, [k], "C")]
                fwd[k] += [("a", o, rest, "C"), ("b", o, rest, "S")]
        own[o].append(("f", o, first + heavy([h for h in hub if h != o]), "S"))

    nodes = list(range(len(cores)))
    prog = {}
    for v in nodes:
        prog[v] = own.get(v, []) + ([("x", None, [aide[v]], "H")] if v in aide else []) + fwd.get(v, [])

    def cost(a, b, kind, lane):
        ca, cb = cores[a], cores[b]
        full = CABLE if rack(ca) != rack(cb) else (CHIP if place(ca) == place(cb) else 1.0) * (1.0 if lane == "L" else LANE)
        return full if kind == "f" else full * HALF

    land = {v: {} for v in nodes}
    got = {v: {} for v in nodes}
    for r in R:
        land[r][(r, "a")] = land[r][(r, "b")] = -HOP
    ptr = {v: 0 for v in nodes}
    free = {(v, l): 0.0 for v in nodes for l in "CSH"}
    moved = True
    while moved:
        moved = False
        for v in nodes:
            while ptr[v] < len(prog[v]):
                kind, j, ds, lane = prog[v][ptr[v]]
                if kind != "x":
                    ls = "CS" if lane == "L" else lane
                    need = ["a", "b"] if kind == "f" else [kind]
                    if any((j, p) not in land[v] for p in need):
                        break
                    t = max(land[v][(j, p)] for p in need) + HOP + (COLD if v >= n and ptr[v] == 0 else 0.0)
                    t = max([t] + [free[(v, l)] for l in ls])
                    for d in ds:
                        t += cost(v, d, kind, lane)
                        for p in need:
                            land[d][(j, p)] = t
                        got[d].setdefault(j, {})[kind] = (v, lane)
                    for l in ls:
                        free[(v, l)] = t
                ptr[v] += 1
                moved = True
    order = {}
    for v in R + list(home):
        js = [j for j in range(NE) if (j, "b") in land[v]]
        order[v] = sorted(js, key=lambda j: land[v][(j, "b")])
    return {"cores": cores, "wid": wid, "prog": prog, "order": order, "got": got, "aide": aide, "home": home}


def _bits(m):
    return bin(m).count("1")


def rank_program(g, core, T, topo):
    if "p" not in _CACHE:
        _CACHE["p"] = _plan(T, topo)
    P = _CACHE["p"]
    cores, wid = P["cores"], P["wid"]
    if core not in cores:
        return
    node = cores.index(core)
    rank = T.rank_of(core)
    home = P["home"].get(node)
    S = T.sem
    te, ve, sy, sc = g.tensor, g.vector, g.sync, g.scalar

    def lanes(c):
        ms = [topo.mask(c, o) for o in cores if o != c and topo.mask(c, o)]
        lo, al = ms[0], ms[0]
        for m in ms:
            lo &= m
            al |= m
        return lo, al & ~lo

    def lane(c, tag):
        lo, hi = lanes(c)
        if tag == "L":
            return lo
        if tag == "H":
            return hi
        bs = [b for b in range(lo.bit_length()) if (lo >> b) & 1]
        return sum(1 << b for b in (bs[0::2] if tag == "C" else bs[1::2]))

    got = P["got"][node]

    def adds(j, kind):
        v, tag = got[j][kind]
        return _bits(lane(cores[v], tag))

    def piece(j, kind):
        a = j * WC + (D if kind == "b" else 0)
        b = j * WC + (D if kind == "a" else WC)
        return T.wall[:, a:b]

    def arrived(q, j, kind):
        if j == rank:
            q.wait_ge(S.lw, 32)
        elif "f" in got[j]:
            q.wait_ge(S["a%d" % j], adds(j, "f"))
        else:
            if kind != "b":
                q.wait_ge(S["a%d" % j], adds(j, "a"))
            if kind != "a":
                q.wait_ge(S["b%d" % j], adds(j, "b"))

    sent = [0]

    def put(src, dst, dsts, sem, m):
        ids = []
        for d in dsts:
            rid, pid = topo.addr(cores[d], core)
            ids.append(DstId(rid=rid, pnc=pid))
        g.remote_dma_fused([RemoteDMATransfer(dst_ids=ids, dma_engine_mask=m, remote_sem=sem,
                                              srcs=[src], dsts=[dst for _ in dsts], alu_op=0)], local_sem=S.sent)
        sent[0] += _bits(m)

    if rank is not None:
        w = wid[rank]
        sy.dma_start(T.wall[:, rank * WC:rank * WC + D], T.w1[:, :]).then_inc(S.lw, 16)
        sc.dma_start(T.wall[:, rank * WC + D:(rank + 1) * WC], T.w2[:, :]).then_inc(S.lw, 16)
        sy.dma_start(T.xs[:, 0:w], T.x[:, 0:w]).then_inc(S.lx, 16)

    for kind, j, dsts, tag in P["prog"][node]:
        if kind == "x":
            g.wait_ge(S.lx, 16)
            put(T.xs[:, 0:w], T.xs[:, 0:w], dsts, S.xr, lane(core, tag))
        else:
            arrived(g, j, kind)
            put(piece(j, kind), piece(j, kind), dsts, S[("b%d" if kind == "b" else "a%d") % j], lane(core, tag))
    if rank is None and home is None:
        g.wait_ge(S.sent, sent[0])
        return

    n = wid[rank] if rank is not None else wid[home]
    s = (n // 16) * 8
    order = P["order"][node]
    last = len(order) - 1
    hp = [T.hp0, T.hp1]
    hs = [T.hs0, T.hs1]

    def mm1(i):
        j = order[i]
        arrived(te, j, "a")
        if i < last:
            te.matmul(hp[i % 2][:, 0:n], piece(j, "a"), T.xs[:, 0:n], start=True, stop=True).then_inc(S["p%d" % i], 1)
        else:
            te.matmul(hp[i % 2][:, 0:s], piece(j, "a"), T.xs[:, 0:s], start=True, stop=True).then_inc(S.pa, 1)
            te.matmul(T.hp2[:, 0:n - s], piece(j, "a"), T.xs[:, s:n], start=True, stop=True).then_inc(S.pb, 1)

    def mm2(i):
        j = order[i]
        h = hs[i % 2]
        if j != rank and "f" not in got[j]:
            arrived(te, j, "b")
        if i < last:
            te.wait_ge(S["r%d" % i], 1)
            te.matmul(T.ya[:, 0:s], piece(j, "b"), h[:, 0:s], start=(i == 0), stop=False).then_inc(S["q%d" % i], 1)
            te.matmul(T.yb[:, 0:n - s], piece(j, "b"), h[:, s:n], start=(i == 0), stop=False).then_inc(S["q%d" % i], 1)
        else:
            te.wait_ge(S.ra, 1)
            te.matmul(T.ya[:, 0:s], piece(j, "b"), h[:, 0:s], start=False, stop=True).then_inc(S.qa, 1)
            te.wait_ge(S.rb, 1)
            te.matmul(T.yb[:, 0:n - s], piece(j, "b"), h[:, s:n], start=False, stop=True).then_inc(S.qb, 1)

    if rank is not None:
        te.wait_ge(S.lx, 16)
    else:
        te.wait_ge(S.xr, _bits(lane(cores[home], "H")))
    mm1(0)
    for i in range(last):
        mm1(i + 1)
        mm2(i)
    mm2(last)

    ve.memset(T.zero[:, 0:n], 0.0).then_inc(S.z, 1)
    ve.wait_ge(S.z, 1)
    for i in range(last):
        ve.wait_ge(S["p%d" % i], 1)
        if i >= 2:
            ve.wait_ge(S["q%d" % (i - 2)], 2)
        ve.tensor_tensor(hs[i % 2][:, 0:n], hp[i % 2][:, 0:n], T.zero[:, 0:n], AluOpType.max).then_inc(S["r%d" % i], 1)
    ve.wait_ge(S.pa, 1)
    if last >= 2:
        ve.wait_ge(S["q%d" % (last - 2)], 2)
    ve.tensor_tensor(hs[last % 2][:, 0:s], hp[last % 2][:, 0:s], T.zero[:, 0:s], AluOpType.max).then_inc(S.ra, 1)
    ve.wait_ge(S.pb, 1)
    ve.tensor_tensor(hs[last % 2][:, s:n], T.hp2[:, 0:n - s], T.zero[:, s:n], AluOpType.max).then_inc(S.rb, 1)
    ve.wait_ge(S["q%d" % (last - 1)], 2)
    helped = rank is not None and rank in P["aide"]
    ve.wait_ge(S.qa, 1)
    if helped:
        ve.wait_ge(S.reta, _bits(lane(cores[P["aide"][rank]], "C")))
        ve.tensor_tensor(T.ys[:, 0:s], T.ya[:, 0:s], T.pr[:, 0:s], AluOpType.add).then_inc(S.oa, 1)
    else:
        ve.tensor_copy(T.ys[:, 0:s], T.ya[:, 0:s]).then_inc(S.oa, 1)
    ve.wait_ge(S.qb, 1)
    if helped:
        ve.wait_ge(S.retb, _bits(lane(cores[P["aide"][rank]], "S")))
        ve.tensor_tensor(T.ys[:, s:n], T.yb[:, 0:n - s], T.pr[:, s:n], AluOpType.add).then_inc(S.ob, 1)
    else:
        ve.tensor_copy(T.ys[:, s:n], T.yb[:, 0:n - s]).then_inc(S.ob, 1)

    if rank is None:
        g.wait_ge(S.oa, 1)
        put(T.ys[:, 0:s], T.pr[:, 0:s], [home], S.reta, lane(core, "C"))
        g.wait_ge(S.ob, 1)
        put(T.ys[:, s:n], T.pr[:, s:n], [home], S.retb, lane(core, "S"))
        g.wait_ge(S.sent, sent[0])
        return

    sy.wait_ge(S.oa, 1)
    sy.dma_start(T.y[:, 0:s], T.ys[:, 0:s]).then_inc(S.sa, 16)
    sy.wait_ge(S.sa, 16)
    sc.wait_ge(S.ob, 1)
    sc.dma_start(T.y[:, s:n], T.ys[:, s:n]).then_inc(S.sb, 16)
    sc.wait_ge(S.sb, 16)
    g.wait_ge(S.sent, sent[0])
